import numpy as np
import ml_dtypes


def mxq(x, axis, fmt="e4m3"):
    dtype, down = {"e4m3": (ml_dtypes.float8_e4m3fn, 7), "e5m2": (ml_dtypes.float8_e5m2, 14)}[fmt]
    v = np.moveaxis(np.asarray(x, np.float32).astype(ml_dtypes.bfloat16).astype(np.float64), axis, -1)
    blocks = v.reshape(v.shape[:-1] + (-1, 32))
    amax = np.abs(blocks).max(-1, keepdims=True)
    byte = np.maximum(np.where(amax > 0, np.frexp(amax)[1] - 1 + 127, 0) - down, 1)
    scale = np.exp2(byte - 127.0)
    codes = (blocks / scale).astype(np.float32).astype(dtype).astype(np.float64)
    return np.moveaxis((codes * scale).reshape(v.shape), -1, axis)


WIDE = False


def mx_kscale(k):
    if not WIDE:
        return np.ones(k)
    levels = np.array([24, -24, 12, -12, 0])
    if k % 512:
        return np.exp2(np.random.permutation(np.resize(levels, k // 32))).repeat(32)
    a = np.empty((k // 512, 16))
    for p in range(k // 512):
        a[p, :8] = np.random.permutation(np.resize(levels, 8))
        for g in range(8):
            far = levels[np.abs(levels - a[p, g]) >= 10]
            a[p, g + 8] = far[np.random.randint(len(far))]
    return np.exp2(a.ravel()).repeat(32)


def f64(x):
    return np.asarray(x).astype(np.float64)


E2M1 = np.array([0.0, 0.5, 1.0, 1.5, 2.0, 3.0, 4.0, 6.0, -0.0, -0.5, -1.0, -1.5, -2.0, -3.0, -4.0, -6.0])


def pack_weight(w, fmt):
    k, n = w.shape
    w = f64(np.asarray(w, np.float32).astype(ml_dtypes.bfloat16)).reshape(k // 32, 32, n)
    amax = np.abs(w).max(1)
    if fmt == "e4m3":
        byte = np.frexp(amax)[1] - 1 + 127 - 7
    else:
        mant, ex = np.frexp(amax / 6.0)
        byte = np.where(mant > 0.5, ex, ex - 1) + 127
    byte = np.clip(np.where(amax > 0, byte, 1), 1, 254)
    scaled = (w * np.exp2(127.0 - byte)[:, None, :]).reshape(k, n).astype(np.float32)
    by_word = np.ascontiguousarray(scaled.reshape(k // 512, 128, 4, n).transpose(0, 1, 3, 2))
    if fmt == "e4m3":
        words = by_word.astype(ml_dtypes.float8_e4m3fn).view(np.uint8)
    else:
        c = by_word.astype(ml_dtypes.float4_e2m1fn).view(np.uint8) & 0xF
        words = (c[..., 0::2] | (c[..., 1::2] << 4)).reshape(k // 512, 128, 2 * n)
    return np.ascontiguousarray(words), np.ascontiguousarray(byte.astype(np.uint8).reshape(k // 512, 16, n))


def unpack_weight(words, scales, fmt):
    g, _, n = scales.shape
    words = np.ascontiguousarray(words).reshape(g, 128, n, -1)
    if fmt == "e4m3":
        vals = words.view(ml_dtypes.float8_e4m3fn).astype(np.float64)
    else:
        nib = np.empty((g, 128, n, 4), np.uint8)
        nib[..., 0::2] = words & 0xF
        nib[..., 1::2] = words >> 4
        vals = E2M1[nib]
    vals = vals * np.repeat(np.exp2(scales.astype(np.float64) - 127.0), 8, axis=1)[..., None]
    return vals.transpose(0, 1, 3, 2).reshape(g * 512, n)


def planes(y):
    n, m = y.shape
    v = y.astype(np.float32).astype(ml_dtypes.bfloat16).astype(np.float64).reshape(n // 32, 32, m)
    top = np.abs(v).max(1)
    byte = np.clip(np.where(top > 0, np.frexp(top)[1] - 1 + 127 - 7, 1), 1, 254)
    codes = (v * np.exp2(127.0 - byte)[:, None, :]).reshape(n, m).astype(np.float32).astype(ml_dtypes.float8_e4m3fn).view(np.uint8)
    words = codes.reshape(n // 512, 128, 4, m).transpose(0, 1, 3, 2)
    return np.ascontiguousarray(words), np.ascontiguousarray(byte.astype(np.uint8).reshape(n // 512, 16, m))


K, R, M, N, T = 1024, 512, 512, 1024, 1536


def setup_inputs():
    n = np.random.standard_normal
    u = mx_kscale(R)[:, None]
    s = mx_kscale(K)[:, None]
    w = n((K, R)) / np.sqrt(K) / s * u.T
    w4 = pack_weight(w, "e2m1")
    rest = w - unpack_weight(*w4, "e2m1")
    p_r8 = pack_weight(rest, "e4m3")
    p_wk = pack_weight(n((R, M)) / np.sqrt(R) / u, "e2m1")
    p_wv = pack_weight(n((R, N)) / np.sqrt(R) / u, "e2m1")
    return {
        "x": (n((K, T)) * s).astype(np.float32),
        "w4_words": w4[0],
        "w4_scales": w4[1],
        "r8_words": p_r8[0],
        "r8_scales": p_r8[1],
        "wk_words": p_wk[0],
        "wk_scales": p_wk[1],
        "wv_words": p_wv[0],
        "wv_scales": p_wv[1],
    }


def reference(x, w4_words, w4_scales, r8_words, r8_scales, wk_words, wk_scales, wv_words, wv_scales):
    x_ = mxq(f64(x), 0, "e4m3")
    w4_ = unpack_weight(w4_words, w4_scales, "e2m1")
    r8_ = unpack_weight(r8_words, r8_scales, "e4m3")
    c = w4_.T @ x_ + r8_.T @ x_
    c_ = mxq(c, 0, "e4m3")
    wk_ = unpack_weight(wk_words, wk_scales, "e2m1")
    wv_ = unpack_weight(wv_words, wv_scales, "e2m1")
    kk = wk_.T @ c_
    vv = wv_.T @ c_
    return (kk, vv, c) + planes(c)

@@ -1,0 +1,197 @@
+from contextlib import ExitStack
+
+import concourse.mybir as mybir
+
+K, R, M, N, T = 1024, 512, 512, 1024, 1536
+FLOPS = 2 * T * (2 * K * R + R * M + R * N)
+
+F32 = mybir.dt.float32
+BF16 = mybir.dt.bfloat16
+I32 = mybir.dt.int32
+U8 = mybir.dt.uint8
+FP8X4 = mybir.dt.float8_e4m3fn_x4
+FP4X4 = mybir.dt.float4_e2m1fn_x4
+
+P = 128
+PACK = 4
+K_PASS = P * PACK
+PASSES = K // K_PASS
+CHUNK = 512
+CHUNKS = T // CHUNK
+KK_TILES = M // P
+VV_TILES = N // P
+R8_ROW = 4
+VECTOR_COLS = 320
+
+
+def tile_mix_mla_resid_kernel(
+    tc, x, w4_words, w4_scales, r8_words, r8_scales, wk_words, wk_scales, wv_words, wv_scales,
+    out_0, out_1, out_2, out_3, out_4,
+):
+    nc = tc.nc
+    with ExitStack() as ctx:
+        keep = ctx.enter_context(tc.tile_pool(name="keep", bufs=1))
+        stage = ctx.enter_context(tc.tile_pool(name="stage", bufs=4))
+        psum = ctx.enter_context(tc.psum_pool(name="psum", bufs=8))
+        ctx.enter_context(tc.manual_schedule())
+
+        def kept(name, shape, dtype):
+            return keep.tile(shape, dtype, name=name, align_bytes=64)
+
+        def cols(i):
+            return slice(i * CHUNK, (i + 1) * CHUNK)
+
+        w4_raw = kept("w4_raw", [P, PASSES, 2 * R], U8)
+        r8_raw = kept("r8_raw", [P, PASSES, R], I32)
+        down_scales_raw = kept("down_scales_raw", [P, PASSES, R], U8)
+        w4 = kept("w4", [P, PASSES, PACK, 2 * P], U8)
+        r8 = kept("r8", [P, PASSES, PACK, P], I32)
+        down_scales = kept("down_scales", [P, PASSES, PACK, P], U8)
+        wk = kept("wk", [P, 2 * M], U8)
+        wv = kept("wv", [P, 2 * N], U8)
+        wk_plane = kept("wk_plane", [P, M], U8)
+        wv_plane = kept("wv_plane", [P, N], U8)
+        x_raw = [[kept("x_raw_%d_%d" % (i, a), [P, PACK, CHUNK], F32) for a in range(PASSES)] for i in range(CHUNKS)]
+        x_codes = [[kept("x_codes_%d_%d" % (i, a), [P, CHUNK], I32) for a in range(PASSES)] for i in range(CHUNKS)]
+        x_scales = [[kept("x_scales_%d_%d" % (i, a), [P, CHUNK], U8) for a in range(PASSES)] for i in range(CHUNKS)]
+        c = [kept("c_%d" % i, [P, PACK, CHUNK], F32) for i in range(CHUNKS)]
+        c_codes = kept("c_codes", [P, T], I32)
+        c_scales = kept("c_scales", [P, T], U8)
+        kk = [kept("kk_%d" % i, [P, KK_TILES, CHUNK], F32) for i in range(CHUNKS)]
+        vv = [[kept("vv_%d_%d" % (i, h), [P, KK_TILES, CHUNK], F32) for h in range(2)] for i in range(CHUNKS)]
+
+        def load_x(i, a):
+            rows = x[a * K_PASS:(a + 1) * K_PASS, cols(i)]
+            nc.sync.dma_start(out=x_raw[i][a][:], in_=rows.rearrange("(p j) t -> p j t", j=PACK))
+
+        def load_scales(plane, first_row, scales, which=range(4)):
+            rows = scales.bitcast(I32).rearrange("a (q r) n -> r q a n", r=4)
+            for r in which:
+                nc.sync.dma_start(out=plane[first_row + r:P:32], in_=rows[r])
+
+        def as_plane(tile2d):
+            return tile2d[:].bitcast(I32).rearrange("p (a n) -> p a n", a=1)
+
+        nc.vector.memset(down_scales_raw[:].bitcast(I32), 0)
+        nc.vector.memset(wk_plane[:].bitcast(I32), 0)
+        nc.vector.memset(wv_plane[:].bitcast(I32), 0)
+
+        nc.sync.dma_start(out=w4_raw[:].bitcast(I32), in_=w4_words.bitcast(I32).rearrange("a p n -> p a n"))
+        nc.sync.dma_start(out=r8_raw[:], in_=r8_words.rearrange("a p n i -> p a (n i)").bitcast(I32))
+        load_scales(down_scales_raw[:].bitcast(I32), 0, w4_scales)
+        load_scales(down_scales_raw[:].bitcast(I32), R8_ROW, r8_scales, range(1))
+        load_x(0, 0)
+        load_scales(down_scales_raw[:].bitcast(I32), R8_ROW, r8_scales, range(1, 4))
+        load_x(0, 1)
+        load_x(1, 0)
+        load_x(1, 1)
+        nc.sync.dma_start(out=wk[:].bitcast(I32), in_=wk_words[0].bitcast(I32))
+        load_scales(as_plane(wk_plane), 0, wk_scales)
+        load_x(2, 0)
+        load_x(2, 1)
+        nc.sync.dma_start(out=wv[:].bitcast(I32), in_=wv_words[0].bitcast(I32))
+        load_scales(as_plane(wv_plane), 0, wv_scales)
+
+        def round_rows(src, vector_cols):
+            grouped = stage.tile([P, CHUNK, PACK], BF16, name="grouped", align_bytes=64)
+            shares = [(nc.vector.tensor_copy, slice(0, vector_cols))]
+            if vector_cols < CHUNK:
+                shares.append((nc.scalar.copy, slice(vector_cols, CHUNK)))
+            for engine_copy, share in shares:
+                engine_copy(
+                    out=grouped[:, share, :].rearrange("p (g i) j -> p g j i", i=4),
+                    in_=src[:, :, share].rearrange("p j (g i) -> p g j i", i=4),
+                )
+            return grouped
+
+        def quantize(grouped, codes, scales):
+            nc.vector.quantize_mx(out=codes.bitcast(FP8X4), scales=scales, in_=grouped[:].rearrange("p t j -> p (t j)"))
+
+        def prepare_x(i, a, vector_cols=CHUNK):
+            quantize(round_rows(x_raw[i][a], vector_cols), x_codes[i][a][:], x_scales[i][a][:])
+
+        def prepare_c(i, vector_cols=CHUNK):
+            quantize(round_rows(c[i], vector_cols), c_codes[:, cols(i)], c_scales[:, cols(i)])
+
+        def new_bank():
+            return psum.tile([P, CHUNK], F32, name="bank")
+
+        def down(banks, i, a):
+            for j in range(PACK):
+                rhs = x_codes[i][a][:].bitcast(FP8X4)
+                nc.tensor.matmul_mx(
+                    out=banks[j][:], lhsT=w4[:, a, j, :].bitcast(FP4X4), lhsT_scale=down_scales[:, a, j, :],
+                    rhs=rhs, rhs_scale=x_scales[i][a][:], start=(a == 0), stop=False,
+                )
+                nc.tensor.matmul_mx(
+                    out=banks[j][:], lhsT=r8[:, a, j, :].bitcast(FP8X4), lhsT_scale=down_scales[R8_ROW:P, a, j, :],
+                    rhs=rhs, rhs_scale=x_scales[i][a][:], start=False, stop=(a == PASSES - 1),
+                )
+
+        def store_c(banks, i):
+            for j in range(PACK):
+                nc.scalar.copy(out=c[i][:, j, :], in_=banks[j][:])
+            nc.sync.dma_start(out=out_2[:, cols(i)].rearrange("(p j) t -> p j t", j=PACK), in_=c[i][:])
+
+        def up(words, plane, m, i, dest, engine_copy):
+            bank = new_bank()
+            nc.tensor.matmul_mx(
+                out=bank[:], lhsT=words[:, 2 * P * m:2 * P * (m + 1)].bitcast(FP4X4), lhsT_scale=plane[:, P * m:P * (m + 1)],
+                rhs=c_codes[:, cols(i)].bitcast(FP8X4), rhs_scale=c_scales[:, cols(i)], start=True, stop=True,
+            )
+            engine_copy(out=dest, in_=bank[:])
+
+        both = (nc.vector.tensor_copy, nc.scalar.copy)
+
+        def keys(i, engines):
+            for m in range(KK_TILES):
+                up(wk, wk_plane, m, i, kk[i][:, m, :], engines[m % len(engines)])
+            nc.sync.dma_start(out=out_0[:, cols(i)].rearrange("(m p) t -> p m t", p=P), in_=kk[i][:])
+
+        def values(i, h, engines):
+            for m in range(KK_TILES):
+                up(wv, wv_plane, h * KK_TILES + m, i, vv[i][h][:, m, :], engines[m % len(engines)])
+            nc.sync.dma_start(out=out_1[h * M:(h + 1) * M, cols(i)].rearrange("(m p) t -> p m t", p=P), in_=vv[i][h][:])
+
+        nc.vector.tensor_copy(out=w4[:].rearrange("p a j (m b) -> p a j m b", b=2),
+                              in_=w4_raw[:].rearrange("p a (m j b) -> p a j m b", j=PACK, b=2))
+        nc.vector.tensor_copy(out=r8[:].rearrange("p a j (g i) -> p a g j i", i=4),
+                              in_=r8_raw[:].rearrange("p a (g i j) -> p a g j i", i=4, j=PACK))
+        grouped00 = round_rows(x_raw[0][0], VECTOR_COLS)
+        nc.vector.tensor_copy(out=down_scales[:], in_=down_scales_raw[:].rearrange("p a (m j) -> p a j m", j=PACK))
+        quantize(grouped00, x_codes[0][0][:], x_scales[0][0][:])
+        prepare_x(0, 1, VECTOR_COLS)
+
+        on_vector, on_scalar = both[:1], both[1:]
+        banks0 = [new_bank() for j in range(PACK)]
+        down(banks0, 0, 0)
+        down(banks0, 0, 1)
+        prepare_x(1, 0, VECTOR_COLS)
+        store_c(banks0, 0)
+        prepare_x(1, 1)
+        prepare_c(0, VECTOR_COLS)
+        banks1 = [new_bank() for j in range(PACK)]
+        down(banks1, 1, 0)
+        down(banks1, 1, 1)
+        prepare_x(2, 0)
+        store_c(banks1, 1)
+        keys(0, on_scalar)
+        prepare_x(2, 1)
+        values(0, 0, on_scalar)
+        prepare_c(1)
+        banks2 = [new_bank() for j in range(PACK)]
+        down(banks2, 2, 0)
+        values(0, 1, on_scalar)
+        down(banks2, 2, 1)
+        store_c(banks2, 2)
+        keys(1, on_vector)
+        values(1, 0, both)
+        prepare_c(2, VECTOR_COLS)
+        values(1, 1, both)
+        nc.sync.dma_start(out=out_3[0].rearrange("p t i -> p (t i)").bitcast(I32), in_=c_codes[:])
+        scale_rows = out_4[0].bitcast(I32).rearrange("(q r) n -> r q n", r=4)
+        for r in range(4):
+            nc.sync.dma_start(out=scale_rows[r], in_=c_scales[:].bitcast(I32)[r:P:32])
+        keys(2, both)
+        values(2, 0, both)
+        values(2, 1, both)

@@ -32,7 +32,7 @@ def tile_mix_mla_resid_kernel(
     with ExitStack() as ctx:
         keep = ctx.enter_context(tc.tile_pool(name="keep", bufs=1))
         stage = ctx.enter_context(tc.tile_pool(name="stage", bufs=4))
-        psum = ctx.enter_context(tc.psum_pool(name="psum", bufs=8))
+        psum = ctx.enter_context(tc.psum_pool(name="psum", bufs=1))
         ctx.enter_context(tc.manual_schedule())
 
         def kept(name, shape, dtype):
@@ -43,10 +43,12 @@ def tile_mix_mla_resid_kernel(
 
         w4_raw = kept("w4_raw", [P, PASSES, 2 * R], U8)
         r8_raw = kept("r8_raw", [P, PASSES, R], I32)
-        down_scales_raw = kept("down_scales_raw", [P, PASSES, R], U8)
+        w4_plane_raw = kept("w4_plane_raw", [P, PASSES, R], U8)
+        r8_plane_raw = kept("r8_plane_raw", [P, PASSES, R], U8)
         w4 = kept("w4", [P, PASSES, PACK, 2 * P], U8)
         r8 = kept("r8", [P, PASSES, PACK, P], I32)
-        down_scales = kept("down_scales", [P, PASSES, PACK, P], U8)
+        w4_plane = kept("w4_plane", [P, PASSES, PACK, P], U8)
+        r8_plane = kept("r8_plane", [P, PASSES, PACK, P], U8)
         wk = kept("wk", [P, 2 * M], U8)
         wv = kept("wv", [P, 2 * N], U8)
         wk_plane = kept("wk_plane", [P, M], U8)
@@ -57,8 +59,12 @@ def tile_mix_mla_resid_kernel(
         c = [kept("c_%d" % i, [P, PACK, CHUNK], F32) for i in range(CHUNKS)]
         c_codes = kept("c_codes", [P, T], I32)
         c_scales = kept("c_scales", [P, T], U8)
-        kk = [kept("kk_%d" % i, [P, KK_TILES, CHUNK], F32) for i in range(CHUNKS)]
-        vv = [[kept("vv_%d_%d" % (i, h), [P, KK_TILES, CHUNK], F32) for h in range(2)] for i in range(CHUNKS)]
+        kk = [kept("kk_%d" % n, [P, KK_TILES, w], F32) for n, w in enumerate((2 * CHUNK, CHUNK))]
+
+        def part(tiles, i):
+            start = (i % 2) * CHUNK
+            return tiles[i // 2][:, :, start:start + CHUNK]
+        vv = [kept("vv_%d" % n, [P, T], F32) for n in range(VV_TILES)]
 
         def load_x(i, a):
             rows = x[a * K_PASS:(a + 1) * K_PASS, cols(i)]
@@ -72,17 +78,17 @@ def tile_mix_mla_resid_kernel(
         def as_plane(tile2d):
             return tile2d[:].bitcast(I32).rearrange("p (a n) -> p a n", a=1)
 
-        nc.vector.memset(down_scales_raw[:].bitcast(I32), 0)
+        nc.vector.memset(w4_plane_raw[:].bitcast(I32), 0)
+        nc.vector.memset(r8_plane_raw[:].bitcast(I32), 0)
         nc.vector.memset(wk_plane[:].bitcast(I32), 0)
         nc.vector.memset(wv_plane[:].bitcast(I32), 0)
 
         nc.sync.dma_start(out=w4_raw[:].bitcast(I32), in_=w4_words.bitcast(I32).rearrange("a p n -> p a n"))
-        nc.sync.dma_start(out=r8_raw[:], in_=r8_words.rearrange("a p n i -> p a (n i)").bitcast(I32))
-        load_scales(down_scales_raw[:].bitcast(I32), 0, w4_scales)
-        load_scales(down_scales_raw[:].bitcast(I32), R8_ROW, r8_scales, range(1))
+        load_scales(w4_plane_raw[:].bitcast(I32), 0, w4_scales)
         load_x(0, 0)
-        load_scales(down_scales_raw[:].bitcast(I32), R8_ROW, r8_scales, range(1, 4))
         load_x(0, 1)
+        nc.sync.dma_start(out=r8_raw[:], in_=r8_words.rearrange("a p n i -> p a (n i)").bitcast(I32))
+        load_scales(r8_plane_raw[:].bitcast(I32), R8_ROW, r8_scales)
         load_x(1, 0)
         load_x(1, 1)
         nc.sync.dma_start(out=wk[:].bitcast(I32), in_=wk_words[0].bitcast(I32))
@@ -113,28 +119,29 @@ def tile_mix_mla_resid_kernel(
         def prepare_c(i, vector_cols=CHUNK):
             quantize(round_rows(c[i], vector_cols), c_codes[:, cols(i)], c_scales[:, cols(i)])
 
-        def new_bank():
-            return psum.tile([P, CHUNK], F32, name="bank")
+        def new_bank(slot):
+            return psum.tile([P, CHUNK], F32, name="bank_%d" % slot)
+
+        def down_pass(bank, i, a, j, base, start, stop):
+            lhsT = w4[:, a, j, :].bitcast(FP4X4) if base else r8[:, a, j, :].bitcast(FP8X4)
+            plane = w4_plane[:, a, j, :] if base else r8_plane[R8_ROW:P, a, j, :]
+            nc.tensor.matmul_mx(out=bank[:], lhsT=lhsT, lhsT_scale=plane, rhs=x_codes[i][a][:].bitcast(FP8X4),
+                                rhs_scale=x_scales[i][a][:], start=start, stop=stop)
 
         def down(banks, i, a):
             for j in range(PACK):
-                rhs = x_codes[i][a][:].bitcast(FP8X4)
-                nc.tensor.matmul_mx(
-                    out=banks[j][:], lhsT=w4[:, a, j, :].bitcast(FP4X4), lhsT_scale=down_scales[:, a, j, :],
-                    rhs=rhs, rhs_scale=x_scales[i][a][:], start=(a == 0), stop=False,
-                )
-                nc.tensor.matmul_mx(
-                    out=banks[j][:], lhsT=r8[:, a, j, :].bitcast(FP8X4), lhsT_scale=down_scales[R8_ROW:P, a, j, :],
-                    rhs=rhs, rhs_scale=x_scales[i][a][:], start=False, stop=(a == PASSES - 1),
-                )
+                down_pass(banks[j], i, a, j, True, a == 0, False)
+                down_pass(banks[j], i, a, j, False, False, a == PASSES - 1)
 
-        def store_c(banks, i):
+        def drain_c(banks, i, engines):
             for j in range(PACK):
-                nc.scalar.copy(out=c[i][:, j, :], in_=banks[j][:])
-            nc.sync.dma_start(out=out_2[:, cols(i)].rearrange("(p j) t -> p j t", j=PACK), in_=c[i][:])
+                engines[j % len(engines)](out=c[i][:, j, :], in_=banks[j][:])
 
-        def up(words, plane, m, i, dest, engine_copy):
-            bank = new_bank()
+        def store_c(tokens, src):
+            nc.sync.dma_start(out=out_2[:, tokens].rearrange("(p j) t -> p j t", j=PACK), in_=src)
+
+        def up(words, plane, m, i, slot, dest, engine_copy):
+            bank = new_bank(slot)
             nc.tensor.matmul_mx(
                 out=bank[:], lhsT=words[:, 2 * P * m:2 * P * (m + 1)].bitcast(FP4X4), lhsT_scale=plane[:, P * m:P * (m + 1)],
                 rhs=c_codes[:, cols(i)].bitcast(FP8X4), rhs_scale=c_scales[:, cols(i)], start=True, stop=True,
@@ -143,55 +150,79 @@ def tile_mix_mla_resid_kernel(
 
         both = (nc.vector.tensor_copy, nc.scalar.copy)
 
-        def keys(i, engines):
+        def keys(i, first_slot, engines):
             for m in range(KK_TILES):
-                up(wk, wk_plane, m, i, kk[i][:, m, :], engines[m % len(engines)])
-            nc.sync.dma_start(out=out_0[:, cols(i)].rearrange("(m p) t -> p m t", p=P), in_=kk[i][:])
+                up(wk, wk_plane, m, i, first_slot + m, part(kk, i)[:, m, :], engines[m % len(engines)])
 
-        def values(i, h, engines):
-            for m in range(KK_TILES):
-                up(wv, wv_plane, h * KK_TILES + m, i, vv[i][h][:, m, :], engines[m % len(engines)])
-            nc.sync.dma_start(out=out_1[h * M:(h + 1) * M, cols(i)].rearrange("(m p) t -> p m t", p=P), in_=vv[i][h][:])
+        def store_keys(tokens, src):
+            nc.sync.dma_start(out=out_0[:, tokens].rearrange("(m p) t -> p m t", p=P), in_=src)
+
+        def values(n, i, slot, engine_copy):
+            up(wv, wv_plane, n, i, slot, vv[n][:, cols(i)], engine_copy)
+
+        def deal_plane(plane, raw):
+            nc.vector.tensor_copy(out=plane[:], in_=raw[:].rearrange("p a (m j) -> p a j m", j=PACK))
 
         nc.vector.tensor_copy(out=w4[:].rearrange("p a j (m b) -> p a j m b", b=2),
                               in_=w4_raw[:].rearrange("p a (m j b) -> p a j m b", j=PACK, b=2))
+        deal_plane(w4_plane, w4_plane_raw)
+        prepare_x(0, 0, VECTOR_COLS)
+        prepare_x(0, 1, VECTOR_COLS)
         nc.vector.tensor_copy(out=r8[:].rearrange("p a j (g i) -> p a g j i", i=4),
                               in_=r8_raw[:].rearrange("p a (g i j) -> p a g j i", i=4, j=PACK))
-        grouped00 = round_rows(x_raw[0][0], VECTOR_COLS)
-        nc.vector.tensor_copy(out=down_scales[:], in_=down_scales_raw[:].rearrange("p a (m j) -> p a j m", j=PACK))
-        quantize(grouped00, x_codes[0][0][:], x_scales[0][0][:])
-        prepare_x(0, 1, VECTOR_COLS)
+        deal_plane(r8_plane, r8_plane_raw)
 
         on_vector, on_scalar = both[:1], both[1:]
-        banks0 = [new_bank() for j in range(PACK)]
-        down(banks0, 0, 0)
-        down(banks0, 0, 1)
-        prepare_x(1, 0, VECTOR_COLS)
-        store_c(banks0, 0)
-        prepare_x(1, 1)
+        banks0 = [new_bank(j) for j in range(PACK)]
+        for a in range(PASSES):
+            for j in range(PACK):
+                down_pass(banks0[j], 0, a, j, True, a == 0, False)
+        for j in range(PACK):
+            for a in range(PASSES):
+                down_pass(banks0[j], 0, a, j, False, False, a == PASSES - 1)
+        prepare_x(1, 0)
+        drain_c(banks0, 0, on_scalar)
+        store_c(cols(0), c[0][:])
+        prepare_x(1, 1, VECTOR_COLS)
         prepare_c(0, VECTOR_COLS)
-        banks1 = [new_bank() for j in range(PACK)]
+        banks1 = [new_bank(PACK + j) for j in range(PACK)]
         down(banks1, 1, 0)
         down(banks1, 1, 1)
         prepare_x(2, 0)
-        store_c(banks1, 1)
-        keys(0, on_scalar)
-        prepare_x(2, 1)
-        values(0, 0, on_scalar)
+        drain_c(banks1, 1, on_scalar)
+        store_c(cols(1), c[1][:])
+        keys(0, 0, on_scalar)
         prepare_c(1)
-        banks2 = [new_bank() for j in range(PACK)]
+        words = out_3[0].rearrange("p t i -> p (t i)").bitcast(I32)
+        nc.sync.dma_start(out=words[:, 0:2 * CHUNK], in_=c_codes[:, 0:2 * CHUNK])
+        banks2 = [new_bank(PACK + j) for j in range(PACK)]
         down(banks2, 2, 0)
-        values(0, 1, on_scalar)
+        last_x = round_rows(x_raw[2][1], 192)
+        keys(1, 0, both)
+        store_keys(slice(0, 2 * CHUNK), kk[0][:])
+        quantize(last_x, x_codes[2][1][:], x_scales[2][1][:])
+        early = 3
+        for i in range(CHUNKS - 1):
+            values(0, i, i, both[i])
         down(banks2, 2, 1)
-        store_c(banks2, 2)
-        keys(1, on_vector)
-        values(1, 0, both)
+        drain_c(banks2, 2, both)
+        store_c(cols(2), c[2][:])
         prepare_c(2, VECTOR_COLS)
-        values(1, 1, both)
-        nc.sync.dma_start(out=out_3[0].rearrange("p t i -> p (t i)").bitcast(I32), in_=c_codes[:])
+        for n in range(1, early):
+            for i in range(CHUNKS - 1):
+                values(n, i, (2 * n + i) % PACK, both[1])
+        nc.sync.dma_start(out=words[:, cols(2)], in_=c_codes[:, cols(2)])
         scale_rows = out_4[0].bitcast(I32).rearrange("(q r) n -> r q n", r=4)
         for r in range(4):
             nc.sync.dma_start(out=scale_rows[r], in_=c_scales[:].bitcast(I32)[r:P:32])
-        keys(2, both)
-        values(2, 0, both)
-        values(2, 1, both)
+        for n in range(early):
+            values(n, CHUNKS - 1, PACK + n, both[0])
+            nc.sync.dma_start(out=out_1[n * P:(n + 1) * P, :], in_=vv[n][:])
+        keys(2, 0, both)
+        store_keys(cols(2), kk[1][:])
+        turn = PACK
+        for n in range(early, VV_TILES):
+            for i in range(CHUNKS):
+                values(n, i, turn % 8, both[turn % 2])
+                turn = turn + 1
+            nc.sync.dma_start(out=out_1[n * P:(n + 1) * P, :], in_=vv[n][:])

@@ -20,7 +20,6 @@ CHUNK = 512
 CHUNKS = T // CHUNK
 KK_TILES = M // P
 VV_TILES = N // P
-R8_ROW = 4
 VECTOR_COLS = 320
 
 
@@ -43,60 +42,54 @@ def tile_mix_mla_resid_kernel(
 
         w4_raw = kept("w4_raw", [P, PASSES, 2 * R], U8)
         r8_raw = kept("r8_raw", [P, PASSES, R], I32)
-        w4_plane_raw = kept("w4_plane_raw", [P, PASSES, R], U8)
-        r8_plane_raw = kept("r8_plane_raw", [P, PASSES, R], U8)
+        scale_rows = kept("scale_rows", [P, 2 * PASSES * R + M + N], U8)
+        w4_plane_raw = scale_rows[:, 0:PASSES * R]
+        r8_plane_raw = scale_rows[:, PASSES * R:2 * PASSES * R]
+        wk_plane = scale_rows[:, 2 * PASSES * R:2 * PASSES * R + M]
+        wv_plane = scale_rows[:, 2 * PASSES * R + M:]
         w4 = kept("w4", [P, PASSES, PACK, 2 * P], U8)
         r8 = kept("r8", [P, PASSES, PACK, P], I32)
         w4_plane = kept("w4_plane", [P, PASSES, PACK, P], U8)
         r8_plane = kept("r8_plane", [P, PASSES, PACK, P], U8)
         wk = kept("wk", [P, 2 * M], U8)
         wv = kept("wv", [P, 2 * N], U8)
-        wk_plane = kept("wk_plane", [P, M], U8)
-        wv_plane = kept("wv_plane", [P, N], U8)
         x_raw = [[kept("x_raw_%d_%d" % (i, a), [P, PACK, CHUNK], F32) for a in range(PASSES)] for i in range(CHUNKS)]
         x_codes = [[kept("x_codes_%d_%d" % (i, a), [P, CHUNK], I32) for a in range(PASSES)] for i in range(CHUNKS)]
         x_scales = [[kept("x_scales_%d_%d" % (i, a), [P, CHUNK], U8) for a in range(PASSES)] for i in range(CHUNKS)]
         c = [kept("c_%d" % i, [P, PACK, CHUNK], F32) for i in range(CHUNKS)]
         c_codes = kept("c_codes", [P, T], I32)
         c_scales = kept("c_scales", [P, T], U8)
-        kk = [kept("kk_%d" % n, [P, KK_TILES, w], F32) for n, w in enumerate((2 * CHUNK, CHUNK))]
+        kk = [kept("kk_%d" % n, [P, KK_TILES, w], F32) for n, w in enumerate((CHUNK, 2 * CHUNK))]
 
         def part(tiles, i):
-            start = (i % 2) * CHUNK
-            return tiles[i // 2][:, :, start:start + CHUNK]
-        vv = [kept("vv_%d" % n, [P, T], F32) for n in range(VV_TILES)]
+            start = max(i - 1, 0) * CHUNK
+            return tiles[min(i, 1)][:, :, start:start + CHUNK]
+        vv = [[kept("vv_%d_%d" % (h, n), [P, KK_TILES, w], F32) for n, w in enumerate((CHUNK, 2 * CHUNK))] for h in range(2)]
 
         def load_x(i, a):
             rows = x[a * K_PASS:(a + 1) * K_PASS, cols(i)]
             nc.sync.dma_start(out=x_raw[i][a][:], in_=rows.rearrange("(p j) t -> p j t", j=PACK))
 
-        def load_scales(plane, first_row, scales, which=range(4)):
-            rows = scales.bitcast(I32).rearrange("a (q r) n -> r q a n", r=4)
-            for r in which:
-                nc.sync.dma_start(out=plane[first_row + r:P:32], in_=rows[r])
-
-        def as_plane(tile2d):
-            return tile2d[:].bitcast(I32).rearrange("p (a n) -> p a n", a=1)
-
-        nc.vector.memset(w4_plane_raw[:].bitcast(I32), 0)
-        nc.vector.memset(r8_plane_raw[:].bitcast(I32), 0)
-        nc.vector.memset(wk_plane[:].bitcast(I32), 0)
-        nc.vector.memset(wv_plane[:].bitcast(I32), 0)
+        def load_scales(plane, scales):
+            rows = scales.bitcast(I32).rearrange("a q n -> q a n")
+            nc.sync.dma_start(out=plane.bitcast(I32)[0:16].rearrange("q (a n) -> q a n", a=rows.shape[1]), in_=rows)
 
         nc.sync.dma_start(out=w4_raw[:].bitcast(I32), in_=w4_words.bitcast(I32).rearrange("a p n -> p a n"))
-        load_scales(w4_plane_raw[:].bitcast(I32), 0, w4_scales)
+        for plane, scales in ((w4_plane_raw, w4_scales), (r8_plane_raw, r8_scales), (wk_plane, wk_scales), (wv_plane, wv_scales)):
+            nc.vector.memset(plane.bitcast(I32), 0)
+            load_scales(plane, scales)
         load_x(0, 0)
+        for quadrant in range(1, 4):
+            nc.sync.dma_start(out=scale_rows[:].bitcast(I32)[32 * quadrant:32 * quadrant + 4],
+                              in_=scale_rows[:].bitcast(I32)[4 * quadrant:4 * quadrant + 4])
         load_x(0, 1)
         nc.sync.dma_start(out=r8_raw[:], in_=r8_words.rearrange("a p n i -> p a (n i)").bitcast(I32))
-        load_scales(r8_plane_raw[:].bitcast(I32), R8_ROW, r8_scales)
         load_x(1, 0)
         load_x(1, 1)
-        nc.sync.dma_start(out=wk[:].bitcast(I32), in_=wk_words[0].bitcast(I32))
-        load_scales(as_plane(wk_plane), 0, wk_scales)
         load_x(2, 0)
+        nc.sync.dma_start(out=wk[:].bitcast(I32), in_=wk_words[0].bitcast(I32))
         load_x(2, 1)
         nc.sync.dma_start(out=wv[:].bitcast(I32), in_=wv_words[0].bitcast(I32))
-        load_scales(as_plane(wv_plane), 0, wv_scales)
 
         def round_rows(src, vector_cols):
             grouped = stage.tile([P, CHUNK, PACK], BF16, name="grouped", align_bytes=64)
@@ -124,7 +117,7 @@ def tile_mix_mla_resid_kernel(
 
         def down_pass(bank, i, a, j, base, start, stop):
             lhsT = w4[:, a, j, :].bitcast(FP4X4) if base else r8[:, a, j, :].bitcast(FP8X4)
-            plane = w4_plane[:, a, j, :] if base else r8_plane[R8_ROW:P, a, j, :]
+            plane = w4_plane[:, a, j, :] if base else r8_plane[:, a, j, :]
             nc.tensor.matmul_mx(out=bank[:], lhsT=lhsT, lhsT_scale=plane, rhs=x_codes[i][a][:].bitcast(FP8X4),
                                 rhs_scale=x_scales[i][a][:], start=start, stop=stop)
 
@@ -157,22 +150,29 @@ def tile_mix_mla_resid_kernel(
         def store_keys(tokens, src):
             nc.sync.dma_start(out=out_0[:, tokens].rearrange("(m p) t -> p m t", p=P), in_=src)
 
-        def values(n, i, slot, engine_copy):
-            up(wv, wv_plane, n, i, slot, vv[n][:, cols(i)], engine_copy)
+        def values(h, i, first_slot, engines):
+            for m in range(KK_TILES):
+                up(wv, wv_plane, h * KK_TILES + m, i, first_slot + m, part(vv[h], i)[:, m, :], engines[m % len(engines)])
+
+        def store_values(h, tokens, src):
+            nc.sync.dma_start(out=out_1[h * M:(h + 1) * M, tokens].rearrange("(m p) t -> p m t", p=P), in_=src)
 
         def deal_plane(plane, raw):
-            nc.vector.tensor_copy(out=plane[:], in_=raw[:].rearrange("p a (m j) -> p a j m", j=PACK))
+            nc.vector.tensor_copy(out=plane[:], in_=raw.rearrange("p (a m j) -> p a j m", a=PASSES, j=PACK))
 
         nc.vector.tensor_copy(out=w4[:].rearrange("p a j (m b) -> p a j m b", b=2),
                               in_=w4_raw[:].rearrange("p a (m j b) -> p a j m b", j=PACK, b=2))
+        first_x = round_rows(x_raw[0][0], VECTOR_COLS)
         deal_plane(w4_plane, w4_plane_raw)
-        prepare_x(0, 0, VECTOR_COLS)
+        quantize(first_x, x_codes[0][0][:], x_scales[0][0][:])
+        deal_plane(r8_plane, r8_plane_raw)
         prepare_x(0, 1, VECTOR_COLS)
         nc.vector.tensor_copy(out=r8[:].rearrange("p a j (g i) -> p a g j i", i=4),
                               in_=r8_raw[:].rearrange("p a (g i j) -> p a g j i", i=4, j=PACK))
-        deal_plane(r8_plane, r8_plane_raw)
 
         on_vector, on_scalar = both[:1], both[1:]
+        words = out_3[0].rearrange("p t i -> p (t i)").bitcast(I32)
+        rest = slice(CHUNK, T)
         banks0 = [new_bank(j) for j in range(PACK)]
         for a in range(PASSES):
             for j in range(PACK):
@@ -185,6 +185,7 @@ def tile_mix_mla_resid_kernel(
         store_c(cols(0), c[0][:])
         prepare_x(1, 1, VECTOR_COLS)
         prepare_c(0, VECTOR_COLS)
+        nc.sync.dma_start(out=words[:, cols(0)], in_=c_codes[:, cols(0)])
         banks1 = [new_bank(PACK + j) for j in range(PACK)]
         down(banks1, 1, 0)
         down(banks1, 1, 1)
@@ -192,37 +193,25 @@ def tile_mix_mla_resid_kernel(
         drain_c(banks1, 1, on_scalar)
         store_c(cols(1), c[1][:])
         keys(0, 0, on_scalar)
+        store_keys(cols(0), kk[0][:])
+        prepare_x(2, 1)
         prepare_c(1)
-        words = out_3[0].rearrange("p t i -> p (t i)").bitcast(I32)
-        nc.sync.dma_start(out=words[:, 0:2 * CHUNK], in_=c_codes[:, 0:2 * CHUNK])
         banks2 = [new_bank(PACK + j) for j in range(PACK)]
-        down(banks2, 2, 0)
-        last_x = round_rows(x_raw[2][1], 192)
-        keys(1, 0, both)
-        store_keys(slice(0, 2 * CHUNK), kk[0][:])
-        quantize(last_x, x_codes[2][1][:], x_scales[2][1][:])
-        early = 3
-        for i in range(CHUNKS - 1):
-            values(0, i, i, both[i])
-        down(banks2, 2, 1)
-        drain_c(banks2, 2, both)
+        for h in range(2):
+            values(h, 0, 0, both if h else on_scalar)
+            store_values(h, cols(0), vv[h][0][:])
+            down(banks2, 2, h)
+        drain_c(banks2, 2, on_vector)
         store_c(cols(2), c[2][:])
-        prepare_c(2, VECTOR_COLS)
-        for n in range(1, early):
-            for i in range(CHUNKS - 1):
-                values(n, i, (2 * n + i) % PACK, both[1])
-        nc.sync.dma_start(out=words[:, cols(2)], in_=c_codes[:, cols(2)])
-        scale_rows = out_4[0].bitcast(I32).rearrange("(q r) n -> r q n", r=4)
+        keys(1, 0, on_scalar)
+        prepare_c(2)
+        nc.sync.dma_start(out=words[:, rest], in_=c_codes[:, rest])
+        out_rows = out_4[0].bitcast(I32).rearrange("(q r) n -> r q n", r=4)
         for r in range(4):
-            nc.sync.dma_start(out=scale_rows[r], in_=c_scales[:].bitcast(I32)[r:P:32])
-        for n in range(early):
-            values(n, CHUNKS - 1, PACK + n, both[0])
-            nc.sync.dma_start(out=out_1[n * P:(n + 1) * P, :], in_=vv[n][:])
-        keys(2, 0, both)
-        store_keys(cols(2), kk[1][:])
-        turn = PACK
-        for n in range(early, VV_TILES):
-            for i in range(CHUNKS):
-                values(n, i, turn % 8, both[turn % 2])
-                turn = turn + 1
-            nc.sync.dma_start(out=out_1[n * P:(n + 1) * P, :], in_=vv[n][:])
+            nc.sync.dma_start(out=out_rows[r], in_=c_scales[:].bitcast(I32)[r:P:32])
+        keys(2, PACK, both)
+        store_keys(rest, kk[1][:])
+        for h in range(2):
+            values(h, 1, 0, both)
+            values(h, 2, PACK, both)
+            store_values(h, rest, vv[h][1][:])

from contextlib import ExitStack

import concourse.mybir as mybir

K, R, M, N, T = 1024, 512, 512, 1024, 1536
FLOPS = 2 * T * (2 * K * R + R * M + R * N)

F32 = mybir.dt.float32
BF16 = mybir.dt.bfloat16
I32 = mybir.dt.int32
U8 = mybir.dt.uint8
FP8X4 = mybir.dt.float8_e4m3fn_x4
FP4X4 = mybir.dt.float4_e2m1fn_x4

P = 128
PACK = 4
K_PASS = P * PACK
PASSES = K // K_PASS
CHUNK = 512
CHUNKS = T // CHUNK
KK_TILES = M // P
VV_TILES = N // P
VECTOR_COLS = 320


def tile_mix_mla_resid_kernel(
    tc, x, w4_words, w4_scales, r8_words, r8_scales, wk_words, wk_scales, wv_words, wv_scales,
    out_0, out_1, out_2, out_3, out_4,
):
    nc = tc.nc
    with ExitStack() as ctx:
        keep = ctx.enter_context(tc.tile_pool(name="keep", bufs=1))
        stage = ctx.enter_context(tc.tile_pool(name="stage", bufs=4))
        psum = ctx.enter_context(tc.psum_pool(name="psum", bufs=1))
        ctx.enter_context(tc.manual_schedule())

        def kept(name, shape, dtype):
            return keep.tile(shape, dtype, name=name, align_bytes=64)

        def cols(i):
            return slice(i * CHUNK, (i + 1) * CHUNK)

        w4_raw = kept("w4_raw", [P, PASSES, 2 * R], U8)
        r8_raw = kept("r8_raw", [P, PASSES, R], I32)
        scale_rows = kept("scale_rows", [P, 2 * PASSES * R + M + N], U8)
        w4_plane_raw = scale_rows[:, 0:PASSES * R]
        r8_plane_raw = scale_rows[:, PASSES * R:2 * PASSES * R]
        wk_plane = scale_rows[:, 2 * PASSES * R:2 * PASSES * R + M]
        wv_plane = scale_rows[:, 2 * PASSES * R + M:]
        w4 = kept("w4", [P, PASSES, PACK, 2 * P], U8)
        r8 = kept("r8", [P, PASSES, PACK, P], I32)
        w4_plane = kept("w4_plane", [P, PASSES, PACK, P], U8)
        r8_plane = kept("r8_plane", [P, PASSES, PACK, P], U8)
        wk = kept("wk", [P, 2 * M], U8)
        wv = kept("wv", [P, 2 * N], U8)
        x_raw = [[kept("x_raw_%d_%d" % (i, a), [P, PACK, CHUNK], F32) for a in range(PASSES)] for i in range(CHUNKS)]
        x_codes = [[kept("x_codes_%d_%d" % (i, a), [P, CHUNK], I32) for a in range(PASSES)] for i in range(CHUNKS)]
        x_scales = [[kept("x_scales_%d_%d" % (i, a), [P, CHUNK], U8) for a in range(PASSES)] for i in range(CHUNKS)]
        c = [kept("c_%d" % i, [P, PACK, CHUNK], F32) for i in range(CHUNKS)]
        c_codes = kept("c_codes", [P, T], I32)
        c_scales = kept("c_scales", [P, T], U8)
        kk = [kept("kk_%d" % n, [P, KK_TILES, w], F32) for n, w in enumerate((CHUNK, 2 * CHUNK))]

        def part(tiles, i):
            start = max(i - 1, 0) * CHUNK
            return tiles[min(i, 1)][:, :, start:start + CHUNK]
        vv = [[kept("vv_%d_%d" % (h, n), [P, KK_TILES, w], F32) for n, w in enumerate((CHUNK, 2 * CHUNK))] for h in range(2)]

        def load_x(i, a):
            rows = x[a * K_PASS:(a + 1) * K_PASS, cols(i)]
            nc.sync.dma_start(out=x_raw[i][a][:], in_=rows.rearrange("(p j) t -> p j t", j=PACK))

        def load_scales(plane, scales):
            rows = scales.bitcast(I32).rearrange("a q n -> q a n")
            nc.sync.dma_start(out=plane.bitcast(I32)[0:16].rearrange("q (a n) -> q a n", a=rows.shape[1]), in_=rows)

        nc.sync.dma_start(out=w4_raw[:].bitcast(I32), in_=w4_words.bitcast(I32).rearrange("a p n -> p a n"))
        for plane, scales in ((w4_plane_raw, w4_scales), (r8_plane_raw, r8_scales), (wk_plane, wk_scales), (wv_plane, wv_scales)):
            nc.vector.memset(plane.bitcast(I32), 0)
            load_scales(plane, scales)
        load_x(0, 0)
        for quadrant in range(1, 4):
            nc.sync.dma_start(out=scale_rows[:].bitcast(I32)[32 * quadrant:32 * quadrant + 4],
                              in_=scale_rows[:].bitcast(I32)[4 * quadrant:4 * quadrant + 4])
        load_x(0, 1)
        nc.sync.dma_start(out=r8_raw[:], in_=r8_words.rearrange("a p n i -> p a (n i)").bitcast(I32))
        load_x(1, 0)
        load_x(1, 1)
        load_x(2, 0)
        nc.sync.dma_start(out=wk[:].bitcast(I32), in_=wk_words[0].bitcast(I32))
        load_x(2, 1)
        nc.sync.dma_start(out=wv[:].bitcast(I32), in_=wv_words[0].bitcast(I32))

        def round_rows(src, vector_cols):
            grouped = stage.tile([P, CHUNK, PACK], BF16, name="grouped", align_bytes=64)
            shares = [(nc.vector.tensor_copy, slice(0, vector_cols))]
            if vector_cols < CHUNK:
                shares.append((nc.scalar.copy, slice(vector_cols, CHUNK)))
            for engine_copy, share in shares:
                engine_copy(
                    out=grouped[:, share, :].rearrange("p (g i) j -> p g j i", i=4),
                    in_=src[:, :, share].rearrange("p j (g i) -> p g j i", i=4),
                )
            return grouped

        def quantize(grouped, codes, scales):
            nc.vector.quantize_mx(out=codes.bitcast(FP8X4), scales=scales, in_=grouped[:].rearrange("p t j -> p (t j)"))

        def prepare_x(i, a, vector_cols=CHUNK):
            quantize(round_rows(x_raw[i][a], vector_cols), x_codes[i][a][:], x_scales[i][a][:])

        def prepare_c(i, vector_cols=CHUNK):
            quantize(round_rows(c[i], vector_cols), c_codes[:, cols(i)], c_scales[:, cols(i)])

        def new_bank(slot):
            return psum.tile([P, CHUNK], F32, name="bank_%d" % slot)

        def down_pass(bank, i, a, j, base, start, stop):
            lhsT = w4[:, a, j, :].bitcast(FP4X4) if base else r8[:, a, j, :].bitcast(FP8X4)
            plane = w4_plane[:, a, j, :] if base else r8_plane[:, a, j, :]
            nc.tensor.matmul_mx(out=bank[:], lhsT=lhsT, lhsT_scale=plane, rhs=x_codes[i][a][:].bitcast(FP8X4),
                                rhs_scale=x_scales[i][a][:], start=start, stop=stop)

        def down(banks, i, a):
            for j in range(PACK):
                down_pass(banks[j], i, a, j, True, a == 0, False)
                down_pass(banks[j], i, a, j, False, False, a == PASSES - 1)

        def drain_c(banks, i, engines):
            for j in range(PACK):
                engines[j % len(engines)](out=c[i][:, j, :], in_=banks[j][:])

        def store_c(tokens, src):
            nc.sync.dma_start(out=out_2[:, tokens].rearrange("(p j) t -> p j t", j=PACK), in_=src)

        def up(words, plane, m, i, slot, dest, engine_copy):
            bank = new_bank(slot)
            nc.tensor.matmul_mx(
                out=bank[:], lhsT=words[:, 2 * P * m:2 * P * (m + 1)].bitcast(FP4X4), lhsT_scale=plane[:, P * m:P * (m + 1)],
                rhs=c_codes[:, cols(i)].bitcast(FP8X4), rhs_scale=c_scales[:, cols(i)], start=True, stop=True,
            )
            engine_copy(out=dest, in_=bank[:])

        both = (nc.vector.tensor_copy, nc.scalar.copy)

        def keys(i, first_slot, engines):
            for m in range(KK_TILES):
                up(wk, wk_plane, m, i, first_slot + m, part(kk, i)[:, m, :], engines[m % len(engines)])

        def store_keys(tokens, src):
            nc.sync.dma_start(out=out_0[:, tokens].rearrange("(m p) t -> p m t", p=P), in_=src)

        def values(h, i, first_slot, engines):
            for m in range(KK_TILES):
                up(wv, wv_plane, h * KK_TILES + m, i, first_slot + m, part(vv[h], i)[:, m, :], engines[m % len(engines)])

        def store_values(h, tokens, src):
            nc.sync.dma_start(out=out_1[h * M:(h + 1) * M, tokens].rearrange("(m p) t -> p m t", p=P), in_=src)

        def deal_plane(plane, raw):
            nc.vector.tensor_copy(out=plane[:], in_=raw.rearrange("p (a m j) -> p a j m", a=PASSES, j=PACK))

        nc.vector.tensor_copy(out=w4[:].rearrange("p a j (m b) -> p a j m b", b=2),
                              in_=w4_raw[:].rearrange("p a (m j b) -> p a j m b", j=PACK, b=2))
        first_x = round_rows(x_raw[0][0], VECTOR_COLS)
        deal_plane(w4_plane, w4_plane_raw)
        quantize(first_x, x_codes[0][0][:], x_scales[0][0][:])
        deal_plane(r8_plane, r8_plane_raw)
        prepare_x(0, 1, VECTOR_COLS)
        nc.vector.tensor_copy(out=r8[:].rearrange("p a j (g i) -> p a g j i", i=4),
                              in_=r8_raw[:].rearrange("p a (g i j) -> p a g j i", i=4, j=PACK))

        on_vector, on_scalar = both[:1], both[1:]
        words = out_3[0].rearrange("p t i -> p (t i)").bitcast(I32)
        rest = slice(CHUNK, T)
        banks0 = [new_bank(j) for j in range(PACK)]
        for a in range(PASSES):
            for j in range(PACK):
                down_pass(banks0[j], 0, a, j, True, a == 0, False)
        for j in range(PACK):
            for a in range(PASSES):
                down_pass(banks0[j], 0, a, j, False, False, a == PASSES - 1)
        prepare_x(1, 0)
        drain_c(banks0, 0, on_scalar)
        store_c(cols(0), c[0][:])
        prepare_x(1, 1, VECTOR_COLS)
        prepare_c(0, VECTOR_COLS)
        nc.sync.dma_start(out=words[:, cols(0)], in_=c_codes[:, cols(0)])
        banks1 = [new_bank(PACK + j) for j in range(PACK)]
        down(banks1, 1, 0)
        down(banks1, 1, 1)
        prepare_x(2, 0)
        drain_c(banks1, 1, on_scalar)
        store_c(cols(1), c[1][:])
        keys(0, 0, on_scalar)
        store_keys(cols(0), kk[0][:])
        prepare_x(2, 1)
        prepare_c(1)
        banks2 = [new_bank(PACK + j) for j in range(PACK)]
        for h in range(2):
            values(h, 0, 0, both if h else on_scalar)
            store_values(h, cols(0), vv[h][0][:])
            down(banks2, 2, h)
        drain_c(banks2, 2, on_vector)
        store_c(cols(2), c[2][:])
        keys(1, 0, on_scalar)
        prepare_c(2)
        nc.sync.dma_start(out=words[:, rest], in_=c_codes[:, rest])
        out_rows = out_4[0].bitcast(I32).rearrange("(q r) n -> r q n", r=4)
        for r in range(4):
            nc.sync.dma_start(out=out_rows[r], in_=c_scales[:].bitcast(I32)[r:P:32])
        keys(2, PACK, both)
        store_keys(rest, kk[1][:])
        for h in range(2):
            values(h, 1, 0, both)
            values(h, 2, PACK, both)
            store_values(h, rest, vv[h][1][:])
